import numpy as np
import ml_dtypes


def mxq(x, axis, fmt="e4m3"):
    dtype, down = {"e4m3": (ml_dtypes.float8_e4m3fn, 7), "e5m2": (ml_dtypes.float8_e5m2, 14)}[fmt]
    v = np.moveaxis(np.asarray(x, np.float32).astype(ml_dtypes.bfloat16).astype(np.float64), axis, -1)
    blocks = v.reshape(v.shape[:-1] + (-1, 32))
    amax = np.abs(blocks).max(-1, keepdims=True)
    byte = np.maximum(np.where(amax > 0, np.frexp(amax)[1] - 1 + 127, 0) - down, 1)
    scale = np.exp2(byte - 127.0)
    codes = (blocks / scale).astype(np.float32).astype(dtype).astype(np.float64)
    return np.moveaxis((codes * scale).reshape(v.shape), -1, axis)


WIDE = False


def mx_kscale(k):
    if not WIDE:
        return np.ones(k)
    levels = np.array([10, -10, 5, -5, 0])
    if k % 512:
        return np.exp2(np.random.permutation(np.resize(levels, k // 32))).repeat(32)
    a = np.empty((k // 512, 16))
    for p in range(k // 512):
        a[p, :8] = np.random.permutation(np.resize(levels, 8))
        for g in range(8):
            far = levels[np.abs(levels - a[p, g]) >= 10]
            a[p, g + 8] = far[np.random.randint(len(far))]
    return np.exp2(a.ravel()).repeat(32)


def f64(x):
    return np.asarray(x).astype(np.float64)


def striped8(idx):
    return np.asarray(idx).reshape(8, -1, 16).transpose(0, 2, 1).reshape(128, -1).astype(np.uint16)


def unstriped8(offs):
    return offs.reshape(8, 16, -1).transpose(0, 2, 1).reshape(8, -1).astype(np.int64)


def pick8(x, idx, run):
    r = np.arange(len(x))
    return x[r[:, None], idx[r % (8 * run) // run]]


E2M1 = np.array([0.0, 0.5, 1.0, 1.5, 2.0, 3.0, 4.0, 6.0, -0.0, -0.5, -1.0, -1.5, -2.0, -3.0, -4.0, -6.0])


def pack_weight(w, fmt):
    k, n = w.shape
    w = f64(np.asarray(w, np.float32).astype(ml_dtypes.bfloat16)).reshape(k // 32, 32, n)
    amax = np.abs(w).max(1)
    if fmt == "e4m3":
        byte = np.frexp(amax)[1] - 1 + 127 - 7
    else:
        mant, ex = np.frexp(amax / 6.0)
        byte = np.where(mant > 0.5, ex, ex - 1) + 127
    byte = np.clip(np.where(amax > 0, byte, 1), 1, 254)
    scaled = (w * np.exp2(127.0 - byte)[:, None, :]).reshape(k, n).astype(np.float32)
    by_word = np.ascontiguousarray(scaled.reshape(k // 512, 128, 4, n).transpose(0, 1, 3, 2))
    if fmt == "e4m3":
        words = by_word.astype(ml_dtypes.float8_e4m3fn).view(np.uint8)
    else:
        c = by_word.astype(ml_dtypes.float4_e2m1fn).view(np.uint8) & 0xF
        words = (c[..., 0::2] | (c[..., 1::2] << 4)).reshape(k // 512, 128, 2 * n)
    return np.ascontiguousarray(words), np.ascontiguousarray(byte.astype(np.uint8).reshape(k // 512, 16, n))


def unpack_weight(words, scales, fmt):
    g, _, n = scales.shape
    words = np.ascontiguousarray(words).reshape(g, 128, n, -1)
    if fmt == "e4m3":
        vals = words.view(ml_dtypes.float8_e4m3fn).astype(np.float64)
    else:
        nib = np.empty((g, 128, n, 4), np.uint8)
        nib[..., 0::2] = words & 0xF
        nib[..., 1::2] = words >> 4
        vals = E2M1[nib]
    vals = vals * np.repeat(np.exp2(scales.astype(np.float64) - 127.0), 8, axis=1)[..., None]
    return vals.transpose(0, 1, 3, 2).reshape(g * 512, n)


D, T, I, Q = 512, 1024, 512, 128


def setup_inputs():
    n = np.random.standard_normal
    idx = np.stack([np.random.permutation(T)[:I] for _ in range(8)])
    idx2 = np.stack([np.random.permutation(T)[:I] for _ in range(8)])
    idx3 = np.stack([np.random.permutation(T)[:I] for _ in range(8)])
    idx4 = np.stack([np.random.permutation(T)[:I] for _ in range(8)])
    fd = mx_kscale(D)
    keysp = pack_weight(n((D, T)) / fd[:, None], "e4m3")
    tagsp = pack_weight(n((D, T)) / fd[:, None], "e2m1")
    return {
        "query": (n((D, Q)) * 0.75 / np.sqrt(D) * fd[:, None]).astype(np.float32),
        "query2": (n((D, Q)) * 0.75 / np.sqrt(D) * fd[:, None]).astype(np.float32),
        "keys_words": keysp[0],
        "keys_scales": keysp[1],
        "tags_words": tagsp[0],
        "tags_scales": tagsp[1],
        "offs": striped8(idx),
        "offs2": striped8(idx2),
        "offs3": striped8(idx3),
        "offs4": striped8(idx4),
    }


def reference(query, query2, keys_words, keys_scales, tags_words, tags_scales, offs, offs2, offs3, offs4):
    idx = unstriped8(offs)
    idx2 = unstriped8(offs2)
    idx3 = unstriped8(offs3)
    idx4 = unstriped8(offs4)
    keysu = unpack_weight(keys_words, keys_scales, "e4m3")
    tagsu = unpack_weight(tags_words, tags_scales, "e2m1")
    queryq = mxq(f64(query), 0, "e4m3")
    query2q = mxq(f64(query2), 0, "e4m3")
    a = queryq.T @ keysu + query2q.T @ tagsu
    w = np.maximum(pick8(a, idx, 16), pick8(a, idx2, 16))
    f1 = np.zeros((Q, T))
    f1[np.arange(Q)[:, None], idx3[np.arange(Q) % 128 // 16]] = w
    cc = a + f1
    tc2 = np.max(cc, axis=1, keepdims=True)
    y = np.exp(pick8(cc, idx4, 16) - tc2)
    return y

@@ -1,0 +1,144 @@
+from contextlib import ExitStack
+
+import concourse.mybir as mybir
+
+D, T, I, Q = 512, 1024, 512, 128
+FLOPS = 2 * 2 * D * Q * T
+
+F32 = mybir.dt.float32
+BF16 = mybir.dt.bfloat16
+I32 = mybir.dt.int32
+U32 = mybir.dt.uint32
+U16 = mybir.dt.uint16
+U8 = mybir.dt.uint8
+FP8X4 = mybir.dt.float8_e4m3fn_x4
+FP4X4 = mybir.dt.float4_e2m1fn_x4
+ALU = mybir.AluOpType
+ACT = mybir.ActivationFunctionType
+
+P = 128
+PACK = 4
+WIDTHS = [256, 256, 256, 128, 128]
+KEY_SPLIT = 768
+HALF = I // 2
+LIST_COLS = I // 16
+
+
+def load_scale_rows(queue, plane, rows):
+    for quad in range(4):
+        queue.dma_start(
+            out=plane[32 * quad : 32 * quad + 4, :].bitcast(I32),
+            in_=rows[0, 4 * quad : 4 * quad + 4, :].bitcast(I32),
+        )
+
+
+def quantize_queries(nc, pool, raw, name):
+    grouped = pool.tile([P, Q, PACK], BF16, name=name + "_grouped", align_bytes=64)
+    codes = pool.tile([P, Q], U32, name=name + "_codes", align_bytes=64)
+    scales = pool.tile([P, Q], U8, name=name + "_scales", align_bytes=64)
+    parts = [slice(0, Q // 2), slice(Q // 2, Q)]
+    for cols in parts:
+        nc.vector.tensor_copy(out=grouped[:, cols, :], in_=raw[:, :, cols].rearrange("p j w -> p w j"))
+    for cols in parts:
+        nc.vector.quantize_mx(
+            out=codes[:, cols].bitcast(FP8X4),
+            scales=scales[:, cols],
+            in_=grouped[:, cols, :].rearrange("p w j -> p (w j)"),
+        )
+    return codes, scales
+
+
+def tile_attend_bestahead_parts_kernel(
+    tc, query, query2, keys_words, keys_scales, tags_words, tags_scales, offs, offs2, offs3, offs4, out
+):
+    nc = tc.nc
+    with ExitStack() as ctx:
+        pool = ctx.enter_context(tc.tile_pool(name="held", bufs=1))
+        psum = ctx.enter_context(tc.psum_pool(name="psum", bufs=1))
+
+        list1 = pool.tile([P, LIST_COLS], U16, name="list1")
+        list2 = pool.tile([P, LIST_COLS], U16, name="list2")
+        list3 = pool.tile([P, LIST_COLS], U16, name="list3")
+        list4 = pool.tile([P, LIST_COLS], U16, name="list4")
+        tag_plane = pool.tile([P, T], U8, name="tag_plane", align_bytes=64)
+        key_plane = pool.tile([P, T], U8, name="key_plane", align_bytes=64)
+        tags = pool.tile([P, 2 * T], U8, name="tags", align_bytes=64)
+        keys = [
+            pool.tile([P, w], U32, name="keys%d" % h, align_bytes=64)
+            for h, w in enumerate([KEY_SPLIT, T - KEY_SPLIT])
+        ]
+        raw1 = pool.tile([P, PACK, Q], F32, name="raw1")
+        raw2 = pool.tile([P, PACK, Q], F32, name="raw2")
+        a = pool.tile([P, T], F32, name="a")
+        f1 = pool.tile([P, T], F32, name="f1")
+        cc = pool.tile([P, T], F32, name="cc")
+        neg_max = pool.tile([P, 1], F32, name="neg_max")
+
+        nc.vector.memset(tag_plane[:].bitcast(I32), 0)
+        nc.vector.memset(key_plane[:].bitcast(I32), 0)
+        nc.vector.memset(f1[:], 0.0)
+
+        key_bytes = keys_words[0].rearrange("p n t -> p (n t)")
+        nc.sync.dma_start(out=raw2[:], in_=query2.rearrange("(p j) w -> p j w", j=PACK))
+        load_scale_rows(nc.sync, tag_plane, tags_scales)
+        nc.sync.dma_start(out=tags[:].bitcast(I32), in_=tags_words[0].bitcast(I32))
+        nc.sync.dma_start(out=raw1[:], in_=query.rearrange("(p j) w -> p j w", j=PACK))
+        nc.sync.dma_start(out=keys[0][:].bitcast(I32), in_=key_bytes[:, : PACK * KEY_SPLIT].bitcast(I32))
+        load_scale_rows(nc.sync, key_plane, keys_scales)
+        nc.sync.dma_start(out=keys[1][:].bitcast(I32), in_=key_bytes[:, PACK * KEY_SPLIT :].bitcast(I32))
+        nc.sync.dma_start(list1[:], offs)
+        nc.sync.dma_start(list2[:], offs2)
+        nc.sync.dma_start(list3[:], offs3)
+        nc.sync.dma_start(list4[:], offs4)
+
+        codes2, scales2 = quantize_queries(nc, pool, raw2, "q2")
+        codes1, scales1 = quantize_queries(nc, pool, raw1, "q1")
+
+        starts = [sum(WIDTHS[:g]) for g in range(len(WIDTHS))]
+        banks = [psum.tile([P, w], F32, name="bank%d" % g) for g, w in enumerate(WIDTHS)]
+        for bank, t0, w in zip(banks, starts, WIDTHS):
+            nc.tensor.matmul_mx(
+                out=bank[:],
+                lhsT=codes2[:].bitcast(FP8X4),
+                lhsT_scale=scales2[:],
+                rhs=tags[:, 2 * t0 : 2 * (t0 + w)].bitcast(FP4X4),
+                rhs_scale=tag_plane[:, t0 : t0 + w],
+                start=True,
+                stop=False,
+            )
+        for g, (bank, t0, w) in enumerate(zip(banks, starts, WIDTHS)):
+            h, c0 = divmod(t0, KEY_SPLIT)
+            nc.tensor.matmul_mx(
+                out=bank[:],
+                lhsT=codes1[:].bitcast(FP8X4),
+                lhsT_scale=scales1[:],
+                rhs=keys[h][:, c0 : c0 + w].bitcast(FP8X4),
+                rhs_scale=key_plane[:, t0 : t0 + w],
+                start=False,
+                stop=True,
+            )
+            if g % 2 == 0:
+                nc.vector.tensor_copy(out=a[:, t0 : t0 + w], in_=bank[:])
+            else:
+                nc.scalar.activation(a[:, t0 : t0 + w], bank[:], ACT.Copy)
+
+        first = [pool.tile([P, HALF], F32, name="first%d" % h) for h in range(2)]
+        second = [pool.tile([P, HALF], F32, name="second%d" % h) for h in range(2)]
+        best = [pool.tile([P, HALF], F32, name="best%d" % h) for h in range(2)]
+        halves = [slice(0, LIST_COLS // 2), slice(LIST_COLS // 2, LIST_COLS)]
+
+        nc.vector.tensor_copy(out=first[0][:], in_=a[:].indirect(list1[:, halves[0]]))
+        nc.scalar.activation(second[0][:], a[:].indirect(list2[:, halves[0]]), ACT.Copy)
+        nc.scalar.activation(second[1][:], a[:].indirect(list2[:, halves[1]]), ACT.Copy)
+        nc.scalar.activation(first[1][:], a[:].indirect(list1[:, halves[1]]), ACT.Copy)
+        for h in range(2):
+            nc.vector.tensor_tensor(best[h][:], first[h][:], second[h][:], ALU.max)
+            nc.vector.tensor_copy(out=f1[:].indirect(list3[:, halves[h]]), in_=best[h][:])
+
+        nc.vector.tensor_tensor(cc[:], a[:], f1[:], ALU.add)
+        nc.vector.tensor_reduce(neg_max[:], cc[:], mybir.AxisListType.X, ALU.max, negate=True)
+
+        for h in range(2):
+            y = pool.tile([P, HALF], F32, name="y%d" % h)
+            nc.scalar.activation(y[:], cc[:].indirect(list4[:, halves[h]]), ACT.Exp, bias=neg_max[:])
+            nc.sync.dma_start(out=out[:, h * HALF : (h + 1) * HALF], in_=y[:])

@@ -24,8 +24,8 @@ HALF = I // 2
 LIST_COLS = I // 16
 
 
-def load_scale_rows(queue, plane, rows):
-    for quad in range(4):
+def load_scale_rows(queues, plane, rows):
+    for quad, queue in enumerate(queues):
         queue.dma_start(
             out=plane[32 * quad : 32 * quad + 4, :].bitcast(I32),
             in_=rows[0, 4 * quad : 4 * quad + 4, :].bitcast(I32),
@@ -64,8 +64,8 @@ def tile_attend_bestahead_parts_kernel(
         key_plane = pool.tile([P, T], U8, name="key_plane", align_bytes=64)
         tags = pool.tile([P, 2 * T], U8, name="tags", align_bytes=64)
         keys = [
-            pool.tile([P, w], U32, name="keys%d" % h, align_bytes=64)
-            for h, w in enumerate([KEY_SPLIT, T - KEY_SPLIT])
+            pool.tile([P, width], U32, name="keys%d" % h, align_bytes=64)
+            for h, width in enumerate([KEY_SPLIT, T - KEY_SPLIT])
         ]
         raw1 = pool.tile([P, PACK, Q], F32, name="raw1")
         raw2 = pool.tile([P, PACK, Q], F32, name="raw2")
@@ -80,11 +80,11 @@ def tile_attend_bestahead_parts_kernel(
 
         key_bytes = keys_words[0].rearrange("p n t -> p (n t)")
         nc.sync.dma_start(out=raw2[:], in_=query2.rearrange("(p j) w -> p j w", j=PACK))
-        load_scale_rows(nc.sync, tag_plane, tags_scales)
+        load_scale_rows([nc.sync, nc.sync, nc.scalar, nc.scalar], tag_plane, tags_scales)
         nc.sync.dma_start(out=tags[:].bitcast(I32), in_=tags_words[0].bitcast(I32))
         nc.sync.dma_start(out=raw1[:], in_=query.rearrange("(p j) w -> p j w", j=PACK))
         nc.sync.dma_start(out=keys[0][:].bitcast(I32), in_=key_bytes[:, : PACK * KEY_SPLIT].bitcast(I32))
-        load_scale_rows(nc.sync, key_plane, keys_scales)
+        load_scale_rows([nc.sync] * 4, key_plane, keys_scales)
         nc.sync.dma_start(out=keys[1][:].bitcast(I32), in_=key_bytes[:, PACK * KEY_SPLIT :].bitcast(I32))
         nc.sync.dma_start(list1[:], offs)
         nc.sync.dma_start(list2[:], offs2)
@@ -95,45 +95,47 @@ def tile_attend_bestahead_parts_kernel(
         codes1, scales1 = quantize_queries(nc, pool, raw1, "q1")
 
         starts = [sum(WIDTHS[:g]) for g in range(len(WIDTHS))]
-        banks = [psum.tile([P, w], F32, name="bank%d" % g) for g, w in enumerate(WIDTHS)]
-        for bank, t0, w in zip(banks, starts, WIDTHS):
+        banks = [psum.tile([P, width], F32, name="bank%d" % g) for g, width in enumerate(WIDTHS)]
+        for bank, t0, width in zip(banks, starts, WIDTHS):
             nc.tensor.matmul_mx(
                 out=bank[:],
                 lhsT=codes2[:].bitcast(FP8X4),
                 lhsT_scale=scales2[:],
-                rhs=tags[:, 2 * t0 : 2 * (t0 + w)].bitcast(FP4X4),
-                rhs_scale=tag_plane[:, t0 : t0 + w],
+                rhs=tags[:, 2 * t0 : 2 * (t0 + width)].bitcast(FP4X4),
+                rhs_scale=tag_plane[:, t0 : t0 + width],
                 start=True,
                 stop=False,
             )
-        for g, (bank, t0, w) in enumerate(zip(banks, starts, WIDTHS)):
+        for g, (bank, t0, width) in enumerate(zip(banks, starts, WIDTHS)):
             h, c0 = divmod(t0, KEY_SPLIT)
             nc.tensor.matmul_mx(
                 out=bank[:],
                 lhsT=codes1[:].bitcast(FP8X4),
                 lhsT_scale=scales1[:],
-                rhs=keys[h][:, c0 : c0 + w].bitcast(FP8X4),
-                rhs_scale=key_plane[:, t0 : t0 + w],
+                rhs=keys[h][:, c0 : c0 + width].bitcast(FP8X4),
+                rhs_scale=key_plane[:, t0 : t0 + width],
                 start=False,
                 stop=True,
             )
             if g % 2 == 0:
-                nc.vector.tensor_copy(out=a[:, t0 : t0 + w], in_=bank[:])
+                nc.vector.tensor_copy(out=a[:, t0 : t0 + width], in_=bank[:])
             else:
-                nc.scalar.activation(a[:, t0 : t0 + w], bank[:], ACT.Copy)
+                nc.scalar.activation(a[:, t0 : t0 + width], bank[:], ACT.Copy)
 
         first = [pool.tile([P, HALF], F32, name="first%d" % h) for h in range(2)]
         second = [pool.tile([P, HALF], F32, name="second%d" % h) for h in range(2)]
-        best = [pool.tile([P, HALF], F32, name="best%d" % h) for h in range(2)]
+        w = pool.tile([P, I], F32, name="w")
         halves = [slice(0, LIST_COLS // 2), slice(LIST_COLS // 2, LIST_COLS)]
 
         nc.vector.tensor_copy(out=first[0][:], in_=a[:].indirect(list1[:, halves[0]]))
         nc.scalar.activation(second[0][:], a[:].indirect(list2[:, halves[0]]), ACT.Copy)
         nc.scalar.activation(second[1][:], a[:].indirect(list2[:, halves[1]]), ACT.Copy)
         nc.scalar.activation(first[1][:], a[:].indirect(list1[:, halves[1]]), ACT.Copy)
-        for h in range(2):
-            nc.vector.tensor_tensor(best[h][:], first[h][:], second[h][:], ALU.max)
-            nc.vector.tensor_copy(out=f1[:].indirect(list3[:, halves[h]]), in_=best[h][:])
+        for lo, hi in [(0, 128), (128, 256)]:
+            nc.vector.tensor_tensor(w[:, lo:hi], first[0][:, lo:hi], second[0][:, lo:hi], ALU.max)
+        nc.vector.tensor_copy(out=f1[:].indirect(list3[:, 0:8]), in_=w[:, 0:128])
+        nc.vector.tensor_tensor(w[:, HALF:], first[1][:], second[1][:], ALU.max)
+        nc.vector.tensor_copy(out=f1[:].indirect(list3[:, 8:32]), in_=w[:, 128:512])
 
         nc.vector.tensor_tensor(cc[:], a[:], f1[:], ALU.add)
         nc.vector.tensor_reduce(neg_max[:], cc[:], mybir.AxisListType.X, ALU.max, negate=True)

@@ -20,14 +20,15 @@ P = 128
 PACK = 4
 WIDTHS = [256, 256, 256, 128, 128]
 KEY_SPLIT = 768
+KEY_ROW0 = 4
 HALF = I // 2
 LIST_COLS = I // 16
 
 
-def load_scale_rows(queues, plane, rows):
+def load_scale_rows(queues, plane, row0, rows):
     for quad, queue in enumerate(queues):
         queue.dma_start(
-            out=plane[32 * quad : 32 * quad + 4, :].bitcast(I32),
+            out=plane[32 * quad + row0 : 32 * quad + row0 + 4, :].bitcast(I32),
             in_=rows[0, 4 * quad : 4 * quad + 4, :].bitcast(I32),
         )
 
@@ -80,11 +81,11 @@ def tile_attend_bestahead_parts_kernel(
 
         key_bytes = keys_words[0].rearrange("p n t -> p (n t)")
         nc.sync.dma_start(out=raw2[:], in_=query2.rearrange("(p j) w -> p j w", j=PACK))
-        load_scale_rows([nc.sync, nc.sync, nc.scalar, nc.scalar], tag_plane, tags_scales)
+        load_scale_rows([nc.sync, nc.sync, nc.scalar, nc.scalar], tag_plane, 0, tags_scales)
         nc.sync.dma_start(out=tags[:].bitcast(I32), in_=tags_words[0].bitcast(I32))
         nc.sync.dma_start(out=raw1[:], in_=query.rearrange("(p j) w -> p j w", j=PACK))
         nc.sync.dma_start(out=keys[0][:].bitcast(I32), in_=key_bytes[:, : PACK * KEY_SPLIT].bitcast(I32))
-        load_scale_rows([nc.sync] * 4, key_plane, keys_scales)
+        load_scale_rows([nc.sync] * 4, key_plane, KEY_ROW0, keys_scales)
         nc.sync.dma_start(out=keys[1][:].bitcast(I32), in_=key_bytes[:, PACK * KEY_SPLIT :].bitcast(I32))
         nc.sync.dma_start(list1[:], offs)
         nc.sync.dma_start(list2[:], offs2)
@@ -113,7 +114,7 @@ def tile_attend_bestahead_parts_kernel(
                 lhsT=codes1[:].bitcast(FP8X4),
                 lhsT_scale=scales1[:],
                 rhs=keys[h][:, c0 : c0 + width].bitcast(FP8X4),
-                rhs_scale=key_plane[:, t0 : t0 + width],
+                rhs_scale=key_plane[KEY_ROW0:, t0 : t0 + width],
                 start=False,
                 stop=True,
             )
@@ -137,7 +138,9 @@ def tile_attend_bestahead_parts_kernel(
         nc.vector.tensor_tensor(w[:, HALF:], first[1][:], second[1][:], ALU.max)
         nc.vector.tensor_copy(out=f1[:].indirect(list3[:, 8:32]), in_=w[:, 128:512])
 
-        nc.vector.tensor_tensor(cc[:], a[:], f1[:], ALU.add)
+        nc.gpsimd.tensor_tensor(cc[:, KEY_SPLIT:], a[:, KEY_SPLIT:], f1[:, KEY_SPLIT:], ALU.add)
+        for bank, t0, width in zip(banks[:3], starts, WIDTHS):
+            nc.vector.tensor_tensor(cc[:, t0 : t0 + width], bank[:], f1[:, t0 : t0 + width], ALU.add)
         nc.vector.tensor_reduce(neg_max[:], cc[:], mybir.AxisListType.X, ALU.max, negate=True)
 
         for h in range(2):

from contextlib import ExitStack

import concourse.mybir as mybir

D, T, I, Q = 512, 1024, 512, 128
FLOPS = 2 * 2 * D * Q * T

F32 = mybir.dt.float32
BF16 = mybir.dt.bfloat16
I32 = mybir.dt.int32
U32 = mybir.dt.uint32
U16 = mybir.dt.uint16
U8 = mybir.dt.uint8
FP8X4 = mybir.dt.float8_e4m3fn_x4
FP4X4 = mybir.dt.float4_e2m1fn_x4
ALU = mybir.AluOpType
ACT = mybir.ActivationFunctionType

P = 128
PACK = 4
WIDTHS = [256, 256, 256, 128, 128]
KEY_SPLIT = 768
KEY_ROW0 = 4
HALF = I // 2
LIST_COLS = I // 16


def load_scale_rows(queues, plane, row0, rows):
    for quad, queue in enumerate(queues):
        queue.dma_start(
            out=plane[32 * quad + row0 : 32 * quad + row0 + 4, :].bitcast(I32),
            in_=rows[0, 4 * quad : 4 * quad + 4, :].bitcast(I32),
        )


def quantize_queries(nc, pool, raw, name):
    grouped = pool.tile([P, Q, PACK], BF16, name=name + "_grouped", align_bytes=64)
    codes = pool.tile([P, Q], U32, name=name + "_codes", align_bytes=64)
    scales = pool.tile([P, Q], U8, name=name + "_scales", align_bytes=64)
    parts = [slice(0, Q // 2), slice(Q // 2, Q)]
    for cols in parts:
        nc.vector.tensor_copy(out=grouped[:, cols, :], in_=raw[:, :, cols].rearrange("p j w -> p w j"))
    for cols in parts:
        nc.vector.quantize_mx(
            out=codes[:, cols].bitcast(FP8X4),
            scales=scales[:, cols],
            in_=grouped[:, cols, :].rearrange("p w j -> p (w j)"),
        )
    return codes, scales


def tile_attend_bestahead_parts_kernel(
    tc, query, query2, keys_words, keys_scales, tags_words, tags_scales, offs, offs2, offs3, offs4, out
):
    nc = tc.nc
    with ExitStack() as ctx:
        pool = ctx.enter_context(tc.tile_pool(name="held", bufs=1))
        psum = ctx.enter_context(tc.psum_pool(name="psum", bufs=1))

        list1 = pool.tile([P, LIST_COLS], U16, name="list1")
        list2 = pool.tile([P, LIST_COLS], U16, name="list2")
        list3 = pool.tile([P, LIST_COLS], U16, name="list3")
        list4 = pool.tile([P, LIST_COLS], U16, name="list4")
        tag_plane = pool.tile([P, T], U8, name="tag_plane", align_bytes=64)
        key_plane = pool.tile([P, T], U8, name="key_plane", align_bytes=64)
        tags = pool.tile([P, 2 * T], U8, name="tags", align_bytes=64)
        keys = [
            pool.tile([P, width], U32, name="keys%d" % h, align_bytes=64)
            for h, width in enumerate([KEY_SPLIT, T - KEY_SPLIT])
        ]
        raw1 = pool.tile([P, PACK, Q], F32, name="raw1")
        raw2 = pool.tile([P, PACK, Q], F32, name="raw2")
        a = pool.tile([P, T], F32, name="a")
        f1 = pool.tile([P, T], F32, name="f1")
        cc = pool.tile([P, T], F32, name="cc")
        neg_max = pool.tile([P, 1], F32, name="neg_max")

        nc.vector.memset(tag_plane[:].bitcast(I32), 0)
        nc.vector.memset(key_plane[:].bitcast(I32), 0)
        nc.vector.memset(f1[:], 0.0)

        key_bytes = keys_words[0].rearrange("p n t -> p (n t)")
        nc.sync.dma_start(out=raw2[:], in_=query2.rearrange("(p j) w -> p j w", j=PACK))
        load_scale_rows([nc.sync, nc.sync, nc.scalar, nc.scalar], tag_plane, 0, tags_scales)
        nc.sync.dma_start(out=tags[:].bitcast(I32), in_=tags_words[0].bitcast(I32))
        nc.sync.dma_start(out=raw1[:], in_=query.rearrange("(p j) w -> p j w", j=PACK))
        nc.sync.dma_start(out=keys[0][:].bitcast(I32), in_=key_bytes[:, : PACK * KEY_SPLIT].bitcast(I32))
        load_scale_rows([nc.sync] * 4, key_plane, KEY_ROW0, keys_scales)
        nc.sync.dma_start(out=keys[1][:].bitcast(I32), in_=key_bytes[:, PACK * KEY_SPLIT :].bitcast(I32))
        nc.sync.dma_start(list1[:], offs)
        nc.sync.dma_start(list2[:], offs2)
        nc.sync.dma_start(list3[:], offs3)
        nc.sync.dma_start(list4[:], offs4)

        codes2, scales2 = quantize_queries(nc, pool, raw2, "q2")
        codes1, scales1 = quantize_queries(nc, pool, raw1, "q1")

        starts = [sum(WIDTHS[:g]) for g in range(len(WIDTHS))]
        banks = [psum.tile([P, width], F32, name="bank%d" % g) for g, width in enumerate(WIDTHS)]
        for bank, t0, width in zip(banks, starts, WIDTHS):
            nc.tensor.matmul_mx(
                out=bank[:],
                lhsT=codes2[:].bitcast(FP8X4),
                lhsT_scale=scales2[:],
                rhs=tags[:, 2 * t0 : 2 * (t0 + width)].bitcast(FP4X4),
                rhs_scale=tag_plane[:, t0 : t0 + width],
                start=True,
                stop=False,
            )
        for g, (bank, t0, width) in enumerate(zip(banks, starts, WIDTHS)):
            h, c0 = divmod(t0, KEY_SPLIT)
            nc.tensor.matmul_mx(
                out=bank[:],
                lhsT=codes1[:].bitcast(FP8X4),
                lhsT_scale=scales1[:],
                rhs=keys[h][:, c0 : c0 + width].bitcast(FP8X4),
                rhs_scale=key_plane[KEY_ROW0:, t0 : t0 + width],
                start=False,
                stop=True,
            )
            if g % 2 == 0:
                nc.vector.tensor_copy(out=a[:, t0 : t0 + width], in_=bank[:])
            else:
                nc.scalar.activation(a[:, t0 : t0 + width], bank[:], ACT.Copy)

        first = [pool.tile([P, HALF], F32, name="first%d" % h) for h in range(2)]
        second = [pool.tile([P, HALF], F32, name="second%d" % h) for h in range(2)]
        w = pool.tile([P, I], F32, name="w")
        halves = [slice(0, LIST_COLS // 2), slice(LIST_COLS // 2, LIST_COLS)]

        nc.vector.tensor_copy(out=first[0][:], in_=a[:].indirect(list1[:, halves[0]]))
        nc.scalar.activation(second[0][:], a[:].indirect(list2[:, halves[0]]), ACT.Copy)
        nc.scalar.activation(second[1][:], a[:].indirect(list2[:, halves[1]]), ACT.Copy)
        nc.scalar.activation(first[1][:], a[:].indirect(list1[:, halves[1]]), ACT.Copy)
        for lo, hi in [(0, 128), (128, 256)]:
            nc.vector.tensor_tensor(w[:, lo:hi], first[0][:, lo:hi], second[0][:, lo:hi], ALU.max)
        nc.vector.tensor_copy(out=f1[:].indirect(list3[:, 0:8]), in_=w[:, 0:128])
        nc.vector.tensor_tensor(w[:, HALF:], first[1][:], second[1][:], ALU.max)
        nc.vector.tensor_copy(out=f1[:].indirect(list3[:, 8:32]), in_=w[:, 128:512])

        nc.gpsimd.tensor_tensor(cc[:, KEY_SPLIT:], a[:, KEY_SPLIT:], f1[:, KEY_SPLIT:], ALU.add)
        for bank, t0, width in zip(banks[:3], starts, WIDTHS):
            nc.vector.tensor_tensor(cc[:, t0 : t0 + width], bank[:], f1[:, t0 : t0 + width], ALU.add)
        nc.vector.tensor_reduce(neg_max[:], cc[:], mybir.AxisListType.X, ALU.max, negate=True)

        for h in range(2):
            y = pool.tile([P, HALF], F32, name="y%d" % h)
            nc.scalar.activation(y[:], cc[:].indirect(list4[:, halves[h]]), ACT.Exp, bias=neg_max[:])
            nc.sync.dma_start(out=out[:, h * HALF : (h + 1) * HALF], in_=y[:])
